import numpy as np
import ml_dtypes


def mxq(x, axis, fmt="e4m3"):
    dtype, down = {"e4m3": (ml_dtypes.float8_e4m3fn, 7), "e5m2": (ml_dtypes.float8_e5m2, 14)}[fmt]
    v = np.moveaxis(np.asarray(x, np.float32).astype(ml_dtypes.bfloat16).astype(np.float64), axis, -1)
    blocks = v.reshape(v.shape[:-1] + (-1, 32))
    amax = np.abs(blocks).max(-1, keepdims=True)
    byte = np.maximum(np.where(amax > 0, np.frexp(amax)[1] - 1 + 127, 0) - down, 1)
    scale = np.exp2(byte - 127.0)
    codes = (blocks / scale).astype(np.float32).astype(dtype).astype(np.float64)
    return np.moveaxis((codes * scale).reshape(v.shape), -1, axis)


WIDE = False


def mx_kscale(k):
    if not WIDE:
        return np.ones(k)
    levels = np.array([10, -10, 5, -5, 0])
    if k % 512:
        return np.exp2(np.random.permutation(np.resize(levels, k // 32))).repeat(32)
    a = np.empty((k // 512, 16))
    for p in range(k // 512):
        a[p, :8] = np.random.permutation(np.resize(levels, 8))
        for g in range(8):
            far = levels[np.abs(levels - a[p, g]) >= 10]
            a[p, g + 8] = far[np.random.randint(len(far))]
    return np.exp2(a.ravel()).repeat(32)


def f64(x):
    return np.asarray(x).astype(np.float64)


def striped(idx):
    return np.tile(np.asarray(idx).reshape(-1, 16).T, (8, 1)).astype(np.uint16)


def unstriped(offs):
    return offs[:16].T.reshape(-1).astype(np.int64)


E2M1 = np.array([0.0, 0.5, 1.0, 1.5, 2.0, 3.0, 4.0, 6.0, -0.0, -0.5, -1.0, -1.5, -2.0, -3.0, -4.0, -6.0])


def pack_weight(w, fmt):
    k, n = w.shape
    w = f64(np.asarray(w, np.float32).astype(ml_dtypes.bfloat16)).reshape(k // 32, 32, n)
    amax = np.abs(w).max(1)
    if fmt == "e4m3":
        byte = np.frexp(amax)[1] - 1 + 127 - 7
    else:
        mant, ex = np.frexp(amax / 6.0)
        byte = np.where(mant > 0.5, ex, ex - 1) + 127
    byte = np.clip(np.where(amax > 0, byte, 1), 1, 254)
    scaled = (w * np.exp2(127.0 - byte)[:, None, :]).reshape(k, n).astype(np.float32)
    by_word = np.ascontiguousarray(scaled.reshape(k // 512, 128, 4, n).transpose(0, 1, 3, 2))
    if fmt == "e4m3":
        words = by_word.astype(ml_dtypes.float8_e4m3fn).view(np.uint8)
    else:
        c = by_word.astype(ml_dtypes.float4_e2m1fn).view(np.uint8) & 0xF
        words = (c[..., 0::2] | (c[..., 1::2] << 4)).reshape(k // 512, 128, 2 * n)
    return np.ascontiguousarray(words), np.ascontiguousarray(byte.astype(np.uint8).reshape(k // 512, 16, n))


def unpack_weight(words, scales, fmt):
    g, _, n = scales.shape
    words = np.ascontiguousarray(words).reshape(g, 128, n, -1)
    if fmt == "e4m3":
        vals = words.view(ml_dtypes.float8_e4m3fn).astype(np.float64)
    else:
        nib = np.empty((g, 128, n, 4), np.uint8)
        nib[..., 0::2] = words & 0xF
        nib[..., 1::2] = words >> 4
        vals = E2M1[nib]
    vals = vals * np.repeat(np.exp2(scales.astype(np.float64) - 127.0), 8, axis=1)[..., None]
    return vals.transpose(0, 1, 3, 2).reshape(g * 512, n)


K, T, J, N = 512, 2048, 512, 256


def setup_inputs():
    n = np.random.standard_normal
    idx = np.random.permutation(T)[:J]
    idx2 = np.random.permutation(T)[:J]
    fk = mx_kscale(K)
    xqp = pack_weight(n((K, T)) / fk[:, None], "e2m1")
    wbp = pack_weight(n((K, N)) * 1 / np.sqrt(K) * fk[:, None], "e2m1")
    wmp = pack_weight(n((K, N)) * 1 / np.sqrt(K) * fk[:, None], "e4m3")
    return {
        "xq_words": xqp[0],
        "xq_scales": xqp[1],
        "wb_words": wbp[0],
        "wb_scales": wbp[1],
        "xf": (n((K, T)) / fk[:, None]).astype(np.float32),
        "sh": (np.random.uniform(0.3, 0.7, (1, J))).astype(np.float32),
        "wm_words": wmp[0],
        "wm_scales": wmp[1],
        "offs": striped(idx),
        "offs2": striped(idx2),
    }


def reference(xq_words, xq_scales, wb_words, wb_scales, xf, sh, wm_words, wm_scales, offs, offs2):
    idx = unstriped(offs)
    idx2 = unstriped(offs2)
    xqu = unpack_weight(xq_words, xq_scales, "e2m1")
    wbu = unpack_weight(wb_words, wb_scales, "e2m1")
    wmu = unpack_weight(wm_words, wm_scales, "e4m3")
    z = wbu.T @ xqu
    xm = f64(xf)[:, idx2] + f64(sh) * (f64(xf)[:, idx] - f64(xf)[:, idx2])
    xmq = mxq(xm, 0, "e4m3")
    p = wmu.T @ xmq
    pa = np.zeros((N, T))
    pa[:, idx] = p
    pb = np.zeros((N, T))
    pb[:, idx2] = p
    y = z + pa + pb
    return y

@@ -1,0 +1,228 @@
+from contextlib import ExitStack
+
+import concourse.mybir as mybir
+from concourse.masks import make_identity
+
+K, T, J, N = 512, 2048, 512, 256
+FLOPS = 2 * K * N * (T + J)
+
+F32 = mybir.dt.float32
+BF16 = mybir.dt.bfloat16
+I32 = mybir.dt.int32
+U32 = mybir.dt.uint32
+U16 = mybir.dt.uint16
+U8 = mybir.dt.uint8
+FP8X4 = mybir.dt.float8_e4m3fn_x4
+FP4X4 = mybir.dt.float4_e2m1fn_x4
+MULT = mybir.AluOpType.mult
+ADD = mybir.AluOpType.add
+COPY = mybir.ActivationFunctionType.Copy
+
+P = 128
+PACK = 4
+BANK = 512
+HALF = J // 2
+CHUNKS = T // BANK
+BLOCKS = BANK // P
+
+
+def tile_list_merge_then_spread_kernel(
+    tc, xq_words, xq_scales, wb_words, wb_scales, xf, sh, wm_words, wm_scales, offs, offs2, out
+):
+    nc = tc.nc
+    with ExitStack() as ctx:
+        held = ctx.enter_context(tc.tile_pool(name="held", bufs=1))
+        stage = ctx.enter_context(tc.tile_pool(name="stage", bufs=4))
+        acc = ctx.enter_context(tc.psum_pool(name="acc", bufs=4))
+        rot = ctx.enter_context(tc.psum_pool(name="rot", bufs=4))
+
+        list_a = held.tile([P, J // 16], U16, name="list_a")
+        list_b = held.tile([P, J // 16], U16, name="list_b")
+        sh_col = held.tile([P, PACK], F32, name="sh_col")
+        planes = [held.tile([P, T], F32, name=f"plane{i}") for i in range(PACK)]
+        xq_codes = held.tile([P, 2 * T], U8, name="xq_codes", align_bytes=64)
+        wb_codes = held.tile([P, 2 * N], U8, name="wb_codes", align_bytes=64)
+        wm_codes = held.tile([P, N], U32, name="wm_codes", align_bytes=64)
+        given_scales = held.tile([P, T + 2 * N], U8, name="given_scales", align_bytes=64)
+        xq_sc = given_scales[:, 0:T]
+        wb_sc = given_scales[:, T : T + N]
+        wm_sc = given_scales[:, T + N : T + 2 * N]
+        ident = held.tile([P, P], F32, name="ident")
+        pages = [[held.tile([P, T], F32, name=f"page{nb}{s}") for s in "ab"] for nb in range(2)]
+
+        make_identity(nc, ident[:])
+        nc.gpsimd.memset(given_scales[:].bitcast(I32), 0)
+        for nb in range(2):
+            for s in range(2):
+                nc.vector.memset(pages[nb][s][:], 0.0)
+
+        xf_planes = xf.rearrange("(p i) t -> i p t", i=PACK)
+
+        def load_scales(dst, src):
+            for q in range(4):
+                nc.sync.dma_start(
+                    out=dst[32 * q : 32 * q + 4, :].bitcast(I32), in_=src[0, 4 * q : 4 * q + 4, :].bitcast(I32)
+                )
+
+        nc.sync.dma_start(list_a[:], offs)
+        nc.sync.dma_start(out=sh_col[:], in_=sh.rearrange("o (p c) -> (o p) c", c=PACK))
+        nc.sync.dma_start(list_b[:], offs2)
+        nc.sync.dma_start(out=planes[0][:], in_=xf_planes[0])
+        nc.sync.dma_start(out=planes[1][:], in_=xf_planes[1])
+        nc.sync.dma_start(out=wb_codes[:].bitcast(I32), in_=wb_words[0].bitcast(I32))
+        nc.sync.dma_start(out=xq_codes[:].bitcast(I32), in_=xq_words[0].bitcast(I32))
+        load_scales(wb_sc, wb_scales)
+        nc.sync.dma_start(out=planes[2][:], in_=xf_planes[2])
+        nc.sync.dma_start(out=planes[3][:], in_=xf_planes[3])
+        load_scales(xq_sc, xq_scales)
+        nc.sync.dma_start(
+            out=wm_codes[:].bitcast(I32), in_=wm_words[0].rearrange("p n t -> p (n t)").bitcast(I32)
+        )
+        load_scales(wm_sc, wm_scales)
+
+        sh_bank = rot.tile([P, PACK, P], F32, name="rot")
+        for c in range(PACK):
+            nc.tensor.transpose(sh_bank[:, c, :], sh_col[:, c : c + 1].to_broadcast([P, P]), ident[:])
+        share_a = held.tile([P, J], F32, name="share_a")
+        share_b = held.tile([P, J], F32, name="share_b")
+        sh_in_order = sh_bank[:].rearrange("p c q -> p q c")
+        nc.scalar.activation(
+            share_b[:].rearrange("p (q c) -> p q c", c=PACK), sh_in_order, COPY, bias=1.0, scale=-1.0
+        )
+        nc.scalar.copy(share_a[:].rearrange("p (q c) -> p q c", c=PACK), sh_in_order)
+
+        z = [held.tile([P, T], F32, name=f"z{nb}") for nb in range(2)]
+        for nb in range(2):
+            for c in range(CHUNKS):
+                z_bank = rot.tile([P, BANK], F32, name="rot")
+                nc.tensor.matmul_mx(
+                    z_bank[:],
+                    lhsT=wb_codes[:, 2 * P * nb : 2 * P * (nb + 1)].bitcast(FP4X4),
+                    lhsT_scale=wb_sc[:, P * nb : P * (nb + 1)],
+                    rhs=xq_codes[:, 2 * BANK * c : 2 * BANK * (c + 1)].bitcast(FP4X4),
+                    rhs_scale=xq_sc[:, BANK * c : BANK * (c + 1)],
+                    start=True,
+                    stop=True,
+                )
+                nc.scalar.copy(z[nb][:, BANK * c : BANK * (c + 1)], z_bank[:])
+
+        part_a = held.tile([P, PACK, J], F32, name="part_a")
+        part_b = held.tile([P, PACK, J], F32, name="part_b")
+
+        def gather(part, plane, lst, share, j0, j1):
+            nc.vector.tensor_tensor(
+                part[:, plane, j0:j1],
+                planes[plane][:].indirect(lst[:, j0 // 16 : j1 // 16]),
+                share[:, j0:j1],
+                MULT,
+            )
+
+        merged = [held.tile([P, HALF, PACK], BF16, name=f"merged{h}", align_bytes=64) for h in range(2)]
+        xm_codes = [held.tile([P, HALF], U32, name=f"xm_codes{h}", align_bytes=64) for h in range(2)]
+        xm_sc = [held.tile([P, HALF], U8, name=f"xm_sc{h}", align_bytes=64) for h in range(2)]
+        p_sb = [held.tile([P, J], F32, name=f"p_sb{nb}") for nb in range(2)]
+
+        def merge(h):
+            cols = slice(HALF * h, HALF * (h + 1))
+            nc.vector.tensor_tensor(
+                merged[h][:].rearrange("p (c i) t -> p c t i", i=4),
+                part_a[:, :, cols].rearrange("p t (c i) -> p c t i", i=4),
+                part_b[:, :, cols].rearrange("p t (c i) -> p c t i", i=4),
+                ADD,
+            )
+
+        def quantise(h):
+            nc.vector.quantize_mx(
+                xm_codes[h][:].bitcast(FP8X4), xm_sc[h][:], merged[h][:].rearrange("p j t -> p (j t)")
+            )
+
+        def product(h):
+            for nb in range(2):
+                p_bank = rot.tile([P, HALF], F32, name="rot")
+                nc.tensor.matmul_mx(
+                    p_bank[:],
+                    lhsT=wm_codes[:, P * nb : P * (nb + 1)].bitcast(FP8X4),
+                    lhsT_scale=wm_sc[:, P * nb : P * (nb + 1)],
+                    rhs=xm_codes[h][:].bitcast(FP8X4),
+                    rhs_scale=xm_sc[h][:],
+                    start=True,
+                    stop=True,
+                )
+                nc.scalar.copy(p_sb[nb][:, HALF * h : HALF * (h + 1)], p_bank[:])
+
+        for i in range(PACK - 1):
+            gather(part_a, i, list_a, share_a, 0, J)
+            gather(part_b, i, list_b, share_b, 0, J)
+        last = PACK - 1
+        gather(part_a, last, list_a, share_a, 0, HALF)
+        gather(part_b, last, list_b, share_b, 0, HALF)
+        gather(part_a, last, list_a, share_a, HALF, J)
+        merge(0)
+        gather(part_b, last, list_b, share_b, HALF, J)
+        quantise(0)
+        product(0)
+        merge(1)
+
+        def scatter(nb, s, j0, j1):
+            lst = (list_a, list_b)[s]
+            nc.vector.tensor_copy(
+                pages[nb][s][:].indirect(lst[:, j0 // 16 : j1 // 16]), p_sb[nb][:, j0:j1]
+            )
+
+        scatter(0, 0, 0, HALF)
+        quantise(1)
+        product(1)
+        scatter(0, 1, 0, HALF)
+        scatter(0, 0, HALF, J)
+        scatter(0, 1, HALF, J)
+        scatter(1, 0, 0, J)
+        scatter(1, 1, 0, J)
+
+        def add_turned(bank, src, c, first, final):
+            for u in range(BLOCKS):
+                col = BANK * c + P * u
+                nc.tensor.matmul(
+                    bank[:, u, :],
+                    lhsT=src[:, col : col + P],
+                    rhs=ident[:],
+                    is_transpose=True,
+                    start=(first and u == 0),
+                    stop=(final and u == BLOCKS - 1),
+                )
+
+        def turn_back(bank):
+            turned = stage.tile([P, BLOCKS, P], F32, name="turned")
+            nc.scalar.copy(turned[:], bank[:])
+            back = rot.tile([P, BLOCKS, P], F32, name="rot")
+            for u in range(BLOCKS):
+                nc.tensor.transpose(back[:, u, :], turned[:, u, :], ident[:])
+            return back
+
+        def store(nb, c, result):
+            nc.sync.dma_start(out=out[P * nb : P * (nb + 1), BANK * c : BANK * (c + 1)], in_=result[:])
+
+        sums = [acc.tile([P, BLOCKS, P], F32, name="acc") for c in range(CHUNKS)]
+        for c in range(CHUNKS):
+            add_turned(sums[c], z[0], c, True, False)
+        for c in range(CHUNKS):
+            add_turned(sums[c], pages[0][0], c, False, False)
+        for c in range(CHUNKS):
+            add_turned(sums[c], pages[0][1], c, False, True)
+        for c in range(CHUNKS):
+            back = turn_back(sums[c])
+            result = stage.tile([P, BANK], F32, name="result0")
+            nc.scalar.copy(result[:], back[:].rearrange("p u q -> p (u q)"))
+            store(0, c, result)
+
+        sums = [acc.tile([P, BLOCKS, P], F32, name="acc") for c in range(CHUNKS)]
+        for c in range(CHUNKS):
+            add_turned(sums[c], z[1], c, True, False)
+        for c in range(CHUNKS):
+            add_turned(sums[c], pages[1][0], c, False, True)
+        for c in range(CHUNKS):
+            back = turn_back(sums[c])
+            result = stage.tile([P, BANK], F32, name="result1")
+            nc.vector.tensor_tensor(
+                result[:], back[:].rearrange("p u q -> p (u q)"), pages[1][1][:, BANK * c : BANK * (c + 1)], ADD
+            )
+            store(1, c, result)

@@ -54,7 +54,7 @@ def tile_list_merge_then_spread_kernel(
         nc.gpsimd.memset(given_scales[:].bitcast(I32), 0)
         for nb in range(2):
             for s in range(2):
-                nc.vector.memset(pages[nb][s][:], 0.0)
+                nc.gpsimd.memset(pages[nb][s][:], 0.0)
 
         xf_planes = xf.rearrange("(p i) t -> i p t", i=PACK)
 
@@ -64,10 +64,10 @@ def tile_list_merge_then_spread_kernel(
                     out=dst[32 * q : 32 * q + 4, :].bitcast(I32), in_=src[0, 4 * q : 4 * q + 4, :].bitcast(I32)
                 )
 
-        nc.sync.dma_start(list_a[:], offs)
         nc.sync.dma_start(out=sh_col[:], in_=sh.rearrange("o (p c) -> (o p) c", c=PACK))
-        nc.sync.dma_start(list_b[:], offs2)
+        nc.sync.dma_start(list_a[:], offs)
         nc.sync.dma_start(out=planes[0][:], in_=xf_planes[0])
+        nc.sync.dma_start(list_b[:], offs2)
         nc.sync.dma_start(out=planes[1][:], in_=xf_planes[1])
         nc.sync.dma_start(out=wb_codes[:].bitcast(I32), in_=wb_words[0].bitcast(I32))
         nc.sync.dma_start(out=xq_codes[:].bitcast(I32), in_=xq_words[0].bitcast(I32))
@@ -92,7 +92,8 @@ def tile_list_merge_then_spread_kernel(
         nc.scalar.copy(share_a[:].rearrange("p (q c) -> p q c", c=PACK), sh_in_order)
 
         z = [held.tile([P, T], F32, name=f"z{nb}") for nb in range(2)]
-        for nb in range(2):
+
+        def base(nb):
             for c in range(CHUNKS):
                 z_bank = rot.tile([P, BANK], F32, name="rot")
                 nc.tensor.matmul_mx(
@@ -105,6 +106,8 @@ def tile_list_merge_then_spread_kernel(
                     stop=True,
                 )
                 nc.scalar.copy(z[nb][:, BANK * c : BANK * (c + 1)], z_bank[:])
+
+        base(0)
 
         part_a = held.tile([P, PACK, J], F32, name="part_a")
         part_b = held.tile([P, PACK, J], F32, name="part_b")
@@ -169,14 +172,16 @@ def tile_list_merge_then_spread_kernel(
                 pages[nb][s][:].indirect(lst[:, j0 // 16 : j1 // 16]), p_sb[nb][:, j0:j1]
             )
 
-        scatter(0, 0, 0, HALF)
         quantise(1)
         product(1)
+        scatter(0, 0, 0, HALF)
         scatter(0, 1, 0, HALF)
         scatter(0, 0, HALF, J)
         scatter(0, 1, HALF, J)
         scatter(1, 0, 0, J)
         scatter(1, 1, 0, J)
+
+        base(1)
 
         def add_turned(bank, src, c, first, final):
             for u in range(BLOCKS):
@@ -199,7 +204,7 @@ def tile_list_merge_then_spread_kernel(
             return back
 
         def store(nb, c, result):
-            nc.sync.dma_start(out=out[P * nb : P * (nb + 1), BANK * c : BANK * (c + 1)], in_=result[:])
+            (nc.scalar, nc.sync)[nb].dma_start(out=out[P * nb : P * (nb + 1), BANK * c : BANK * (c + 1)], in_=result[:])
 
         sums = [acc.tile([P, BLOCKS, P], F32, name="acc") for c in range(CHUNKS)]
         for c in range(CHUNKS):
@@ -214,15 +219,18 @@ def tile_list_merge_then_spread_kernel(
             nc.scalar.copy(result[:], back[:].rearrange("p u q -> p (u q)"))
             store(0, c, result)
 
-        sums = [acc.tile([P, BLOCKS, P], F32, name="acc") for c in range(CHUNKS)]
+        partial = []
+
+        def add_first(c):
+            cols = slice(BANK * c, BANK * (c + 1))
+            both = stage.tile([P, BANK], F32, name="both")
+            nc.vector.tensor_tensor(both[:], z[1][:, cols], pages[1][0][:, cols], ADD)
+            partial.append(both)
+
+        add_first(0)
         for c in range(CHUNKS):
-            add_turned(sums[c], z[1], c, True, False)
-        for c in range(CHUNKS):
-            add_turned(sums[c], pages[1][0], c, False, True)
-        for c in range(CHUNKS):
-            back = turn_back(sums[c])
+            if c + 1 < CHUNKS:
+                add_first(c + 1)
             result = stage.tile([P, BANK], F32, name="result1")
-            nc.vector.tensor_tensor(
-                result[:], back[:].rearrange("p u q -> p (u q)"), pages[1][1][:, BANK * c : BANK * (c + 1)], ADD
-            )
+            nc.vector.tensor_tensor(result[:], partial[c][:], pages[1][1][:, BANK * c : BANK * (c + 1)], ADD)
             store(1, c, result)

@@ -20,10 +20,14 @@ COPY = mybir.ActivationFunctionType.Copy
 
 P = 128
 PACK = 4
+QUADRANTS = 4
+PER_COLUMN = 16
+RUN = 4
 BANK = 512
-HALF = J // 2
 CHUNKS = T // BANK
 BLOCKS = BANK // P
+ROW_BLOCKS = N // P
+HALF = J // 2
 
 
 def tile_list_merge_then_spread_kernel(
@@ -32,12 +36,13 @@ def tile_list_merge_then_spread_kernel(
     nc = tc.nc
     with ExitStack() as ctx:
         held = ctx.enter_context(tc.tile_pool(name="held", bufs=1))
-        stage = ctx.enter_context(tc.tile_pool(name="stage", bufs=4))
-        acc = ctx.enter_context(tc.psum_pool(name="acc", bufs=4))
-        rot = ctx.enter_context(tc.psum_pool(name="rot", bufs=4))
+        stage = ctx.enter_context(tc.tile_pool(name="stage", bufs=CHUNKS))
+        acc = ctx.enter_context(tc.psum_pool(name="acc", bufs=CHUNKS))
+        keep = ctx.enter_context(tc.psum_pool(name="keep", bufs=1))
+        rot = ctx.enter_context(tc.psum_pool(name="rot", bufs=3))
 
-        list_a = held.tile([P, J // 16], U16, name="list_a")
-        list_b = held.tile([P, J // 16], U16, name="list_b")
+        list_a = held.tile([P, J // PER_COLUMN], U16, name="list_a")
+        list_b = held.tile([P, J // PER_COLUMN], U16, name="list_b")
         sh_col = held.tile([P, PACK], F32, name="sh_col")
         planes = [held.tile([P, T], F32, name=f"plane{i}") for i in range(PACK)]
         xq_codes = held.tile([P, 2 * T], U8, name="xq_codes", align_bytes=64)
@@ -48,18 +53,18 @@ def tile_list_merge_then_spread_kernel(
         wb_sc = given_scales[:, T : T + N]
         wm_sc = given_scales[:, T + N : T + 2 * N]
         ident = held.tile([P, P], F32, name="ident")
-        pages = [[held.tile([P, T], F32, name=f"page{nb}{s}") for s in "ab"] for nb in range(2)]
+        pages = [[held.tile([P, T], F32, name=f"page{nb}{s}") for s in "ab"] for nb in range(ROW_BLOCKS)]
 
         make_identity(nc, ident[:])
         nc.gpsimd.memset(given_scales[:].bitcast(I32), 0)
-        for nb in range(2):
+        for nb in range(ROW_BLOCKS):
             for s in range(2):
                 nc.gpsimd.memset(pages[nb][s][:], 0.0)
 
         xf_planes = xf.rearrange("(p i) t -> i p t", i=PACK)
 
         def load_scales(dst, src):
-            for q in range(4):
+            for q in range(QUADRANTS):
                 nc.sync.dma_start(
                     out=dst[32 * q : 32 * q + 4, :].bitcast(I32), in_=src[0, 4 * q : 4 * q + 4, :].bitcast(I32)
                 )
@@ -91,23 +96,29 @@ def tile_list_merge_then_spread_kernel(
         )
         nc.scalar.copy(share_a[:].rearrange("p (q c) -> p q c", c=PACK), sh_in_order)
 
-        z = [held.tile([P, T], F32, name=f"z{nb}") for nb in range(2)]
+        z = [held.tile([P, T], F32, name=f"z{nb}") for nb in range(ROW_BLOCKS)]
 
-        def base(nb):
-            for c in range(CHUNKS):
-                z_bank = rot.tile([P, BANK], F32, name="rot")
-                nc.tensor.matmul_mx(
-                    z_bank[:],
-                    lhsT=wb_codes[:, 2 * P * nb : 2 * P * (nb + 1)].bitcast(FP4X4),
-                    lhsT_scale=wb_sc[:, P * nb : P * (nb + 1)],
-                    rhs=xq_codes[:, 2 * BANK * c : 2 * BANK * (c + 1)].bitcast(FP4X4),
-                    rhs_scale=xq_sc[:, BANK * c : BANK * (c + 1)],
-                    start=True,
-                    stop=True,
-                )
-                nc.scalar.copy(z[nb][:, BANK * c : BANK * (c + 1)], z_bank[:])
+        def chunk(c):
+            return slice(BANK * c, BANK * (c + 1))
 
-        base(0)
+        def base(nb, c, z_bank):
+            nc.tensor.matmul_mx(
+                z_bank[:],
+                lhsT=wb_codes[:, 2 * P * nb : 2 * P * (nb + 1)].bitcast(FP4X4),
+                lhsT_scale=wb_sc[:, P * nb : P * (nb + 1)],
+                rhs=xq_codes[:, 2 * BANK * c : 2 * BANK * (c + 1)].bitcast(FP4X4),
+                rhs_scale=xq_sc[:, chunk(c)],
+                start=True,
+                stop=True,
+            )
+
+        def base_to_sbuf(nb, c):
+            z_bank = rot.tile([P, BANK], F32, name="rot")
+            base(nb, c, z_bank)
+            nc.scalar.copy(z[nb][:, chunk(c)], z_bank[:])
+
+        for c in range(CHUNKS):
+            base_to_sbuf(0, c)
 
         part_a = held.tile([P, PACK, J], F32, name="part_a")
         part_b = held.tile([P, PACK, J], F32, name="part_b")
@@ -115,7 +126,7 @@ def tile_list_merge_then_spread_kernel(
         def gather(part, plane, lst, share, j0, j1):
             nc.vector.tensor_tensor(
                 part[:, plane, j0:j1],
-                planes[plane][:].indirect(lst[:, j0 // 16 : j1 // 16]),
+                planes[plane][:].indirect(lst[:, j0 // PER_COLUMN : j1 // PER_COLUMN]),
                 share[:, j0:j1],
                 MULT,
             )
@@ -123,24 +134,24 @@ def tile_list_merge_then_spread_kernel(
         merged = [held.tile([P, HALF, PACK], BF16, name=f"merged{h}", align_bytes=64) for h in range(2)]
         xm_codes = [held.tile([P, HALF], U32, name=f"xm_codes{h}", align_bytes=64) for h in range(2)]
         xm_sc = [held.tile([P, HALF], U8, name=f"xm_sc{h}", align_bytes=64) for h in range(2)]
-        p_sb = [held.tile([P, J], F32, name=f"p_sb{nb}") for nb in range(2)]
+        p_sb = [held.tile([P, J], F32, name=f"p_sb{nb}") for nb in range(ROW_BLOCKS)]
 
         def merge(h):
             cols = slice(HALF * h, HALF * (h + 1))
             nc.vector.tensor_tensor(
-                merged[h][:].rearrange("p (c i) t -> p c t i", i=4),
-                part_a[:, :, cols].rearrange("p t (c i) -> p c t i", i=4),
-                part_b[:, :, cols].rearrange("p t (c i) -> p c t i", i=4),
+                merged[h][:].rearrange("p (c r) i -> p c i r", r=RUN),
+                part_a[:, :, cols].rearrange("p i (c r) -> p c i r", r=RUN),
+                part_b[:, :, cols].rearrange("p i (c r) -> p c i r", r=RUN),
                 ADD,
             )
 
         def quantise(h):
             nc.vector.quantize_mx(
-                xm_codes[h][:].bitcast(FP8X4), xm_sc[h][:], merged[h][:].rearrange("p j t -> p (j t)")
+                xm_codes[h][:].bitcast(FP8X4), xm_sc[h][:], merged[h][:].rearrange("p j i -> p (j i)")
             )
 
         def product(h):
-            for nb in range(2):
+            for nb in range(ROW_BLOCKS):
                 p_bank = rot.tile([P, HALF], F32, name="rot")
                 nc.tensor.matmul_mx(
                     p_bank[:],
@@ -153,10 +164,10 @@ def tile_list_merge_then_spread_kernel(
                 )
                 nc.scalar.copy(p_sb[nb][:, HALF * h : HALF * (h + 1)], p_bank[:])
 
-        for i in range(PACK - 1):
+        last = PACK - 1
+        for i in range(last):
             gather(part_a, i, list_a, share_a, 0, J)
             gather(part_b, i, list_b, share_b, 0, J)
-        last = PACK - 1
         gather(part_a, last, list_a, share_a, 0, HALF)
         gather(part_b, last, list_b, share_b, 0, HALF)
         gather(part_a, last, list_a, share_a, HALF, J)
@@ -165,23 +176,25 @@ def tile_list_merge_then_spread_kernel(
         quantise(0)
         product(0)
         merge(1)
+        quantise(1)
+        product(1)
 
         def scatter(nb, s, j0, j1):
             lst = (list_a, list_b)[s]
             nc.vector.tensor_copy(
-                pages[nb][s][:].indirect(lst[:, j0 // 16 : j1 // 16]), p_sb[nb][:, j0:j1]
+                pages[nb][s][:].indirect(lst[:, j0 // PER_COLUMN : j1 // PER_COLUMN]), p_sb[nb][:, j0:j1]
             )
 
-        quantise(1)
-        product(1)
-        scatter(0, 0, 0, HALF)
-        scatter(0, 1, 0, HALF)
-        scatter(0, 0, HALF, J)
-        scatter(0, 1, HALF, J)
-        scatter(1, 0, 0, J)
-        scatter(1, 1, 0, J)
+        for h in range(2):
+            for s in range(2):
+                scatter(0, s, HALF * h, HALF * (h + 1))
+        for s in range(2):
+            scatter(1, s, 0, J)
 
-        base(1)
+        for c in range(CHUNKS - 1):
+            base_to_sbuf(1, c)
+        z_last = keep.tile([P, BANK], F32, name="z_last")
+        base(1, CHUNKS - 1, z_last)
 
         def add_turned(bank, src, c, first, final):
             for u in range(BLOCKS):
@@ -195,16 +208,8 @@ def tile_list_merge_then_spread_kernel(
                     stop=(final and u == BLOCKS - 1),
                 )
 
-        def turn_back(bank):
-            turned = stage.tile([P, BLOCKS, P], F32, name="turned")
-            nc.scalar.copy(turned[:], bank[:])
-            back = rot.tile([P, BLOCKS, P], F32, name="rot")
-            for u in range(BLOCKS):
-                nc.tensor.transpose(back[:, u, :], turned[:, u, :], ident[:])
-            return back
-
-        def store(nb, c, result):
-            (nc.scalar, nc.sync)[nb].dma_start(out=out[P * nb : P * (nb + 1), BANK * c : BANK * (c + 1)], in_=result[:])
+        def rows(nb, c):
+            return out[P * nb : P * (nb + 1), chunk(c)]
 
         sums = [acc.tile([P, BLOCKS, P], F32, name="acc") for c in range(CHUNKS)]
         for c in range(CHUNKS):
@@ -214,23 +219,20 @@ def tile_list_merge_then_spread_kernel(
         for c in range(CHUNKS):
             add_turned(sums[c], pages[0][1], c, False, True)
         for c in range(CHUNKS):
-            back = turn_back(sums[c])
+            turned = stage.tile([P, BLOCKS, P], F32, name="turned")
+            nc.scalar.copy(turned[:], sums[c][:])
+            back = rot.tile([P, BLOCKS, P], F32, name="rot")
+            for u in range(BLOCKS):
+                nc.tensor.transpose(back[:, u, :], turned[:, u, :], ident[:])
             result = stage.tile([P, BANK], F32, name="result0")
             nc.scalar.copy(result[:], back[:].rearrange("p u q -> p (u q)"))
-            store(0, c, result)
+            nc.scalar.dma_start(out=rows(0, c), in_=result[:])
 
-        partial = []
-
-        def add_first(c):
-            cols = slice(BANK * c, BANK * (c + 1))
-            both = stage.tile([P, BANK], F32, name="both")
-            nc.vector.tensor_tensor(both[:], z[1][:, cols], pages[1][0][:, cols], ADD)
-            partial.append(both)
-
-        add_first(0)
+        partial = [stage.tile([P, BANK], F32, name="both") for c in range(CHUNKS)]
+        for c in range(CHUNKS - 1):
+            nc.gpsimd.tensor_tensor(partial[c][:], z[1][:, chunk(c)], pages[1][0][:, chunk(c)], ADD)
+        nc.vector.tensor_tensor(partial[CHUNKS - 1][:], z_last[:], pages[1][0][:, chunk(CHUNKS - 1)], ADD)
         for c in range(CHUNKS):
-            if c + 1 < CHUNKS:
-                add_first(c + 1)
             result = stage.tile([P, BANK], F32, name="result1")
-            nc.vector.tensor_tensor(result[:], partial[c][:], pages[1][1][:, BANK * c : BANK * (c + 1)], ADD)
-            store(1, c, result)
+            nc.vector.tensor_tensor(result[:], partial[c][:], pages[1][1][:, chunk(c)], ADD)
+            nc.sync.dma_start(out=rows(1, c), in_=result[:])

from contextlib import ExitStack

import concourse.mybir as mybir
from concourse.masks import make_identity

K, T, J, N = 512, 2048, 512, 256
FLOPS = 2 * K * N * (T + J)

F32 = mybir.dt.float32
BF16 = mybir.dt.bfloat16
I32 = mybir.dt.int32
U32 = mybir.dt.uint32
U16 = mybir.dt.uint16
U8 = mybir.dt.uint8
FP8X4 = mybir.dt.float8_e4m3fn_x4
FP4X4 = mybir.dt.float4_e2m1fn_x4
MULT = mybir.AluOpType.mult
ADD = mybir.AluOpType.add
COPY = mybir.ActivationFunctionType.Copy

P = 128
PACK = 4
QUADRANTS = 4
PER_COLUMN = 16
RUN = 4
BANK = 512
CHUNKS = T // BANK
BLOCKS = BANK // P
ROW_BLOCKS = N // P
HALF = J // 2


def tile_list_merge_then_spread_kernel(
    tc, xq_words, xq_scales, wb_words, wb_scales, xf, sh, wm_words, wm_scales, offs, offs2, out
):
    nc = tc.nc
    with ExitStack() as ctx:
        held = ctx.enter_context(tc.tile_pool(name="held", bufs=1))
        stage = ctx.enter_context(tc.tile_pool(name="stage", bufs=CHUNKS))
        acc = ctx.enter_context(tc.psum_pool(name="acc", bufs=CHUNKS))
        keep = ctx.enter_context(tc.psum_pool(name="keep", bufs=1))
        rot = ctx.enter_context(tc.psum_pool(name="rot", bufs=3))

        list_a = held.tile([P, J // PER_COLUMN], U16, name="list_a")
        list_b = held.tile([P, J // PER_COLUMN], U16, name="list_b")
        sh_col = held.tile([P, PACK], F32, name="sh_col")
        planes = [held.tile([P, T], F32, name=f"plane{i}") for i in range(PACK)]
        xq_codes = held.tile([P, 2 * T], U8, name="xq_codes", align_bytes=64)
        wb_codes = held.tile([P, 2 * N], U8, name="wb_codes", align_bytes=64)
        wm_codes = held.tile([P, N], U32, name="wm_codes", align_bytes=64)
        given_scales = held.tile([P, T + 2 * N], U8, name="given_scales", align_bytes=64)
        xq_sc = given_scales[:, 0:T]
        wb_sc = given_scales[:, T : T + N]
        wm_sc = given_scales[:, T + N : T + 2 * N]
        ident = held.tile([P, P], F32, name="ident")
        pages = [[held.tile([P, T], F32, name=f"page{nb}{s}") for s in "ab"] for nb in range(ROW_BLOCKS)]

        make_identity(nc, ident[:])
        nc.gpsimd.memset(given_scales[:].bitcast(I32), 0)
        for nb in range(ROW_BLOCKS):
            for s in range(2):
                nc.gpsimd.memset(pages[nb][s][:], 0.0)

        xf_planes = xf.rearrange("(p i) t -> i p t", i=PACK)

        def load_scales(dst, src):
            for q in range(QUADRANTS):
                nc.sync.dma_start(
                    out=dst[32 * q : 32 * q + 4, :].bitcast(I32), in_=src[0, 4 * q : 4 * q + 4, :].bitcast(I32)
                )

        nc.sync.dma_start(out=sh_col[:], in_=sh.rearrange("o (p c) -> (o p) c", c=PACK))
        nc.sync.dma_start(list_a[:], offs)
        nc.sync.dma_start(out=planes[0][:], in_=xf_planes[0])
        nc.sync.dma_start(list_b[:], offs2)
        nc.sync.dma_start(out=planes[1][:], in_=xf_planes[1])
        nc.sync.dma_start(out=wb_codes[:].bitcast(I32), in_=wb_words[0].bitcast(I32))
        nc.sync.dma_start(out=xq_codes[:].bitcast(I32), in_=xq_words[0].bitcast(I32))
        load_scales(wb_sc, wb_scales)
        nc.sync.dma_start(out=planes[2][:], in_=xf_planes[2])
        nc.sync.dma_start(out=planes[3][:], in_=xf_planes[3])
        load_scales(xq_sc, xq_scales)
        nc.sync.dma_start(
            out=wm_codes[:].bitcast(I32), in_=wm_words[0].rearrange("p n t -> p (n t)").bitcast(I32)
        )
        load_scales(wm_sc, wm_scales)

        sh_bank = rot.tile([P, PACK, P], F32, name="rot")
        for c in range(PACK):
            nc.tensor.transpose(sh_bank[:, c, :], sh_col[:, c : c + 1].to_broadcast([P, P]), ident[:])
        share_a = held.tile([P, J], F32, name="share_a")
        share_b = held.tile([P, J], F32, name="share_b")
        sh_in_order = sh_bank[:].rearrange("p c q -> p q c")
        nc.scalar.activation(
            share_b[:].rearrange("p (q c) -> p q c", c=PACK), sh_in_order, COPY, bias=1.0, scale=-1.0
        )
        nc.scalar.copy(share_a[:].rearrange("p (q c) -> p q c", c=PACK), sh_in_order)

        z = [held.tile([P, T], F32, name=f"z{nb}") for nb in range(ROW_BLOCKS)]

        def chunk(c):
            return slice(BANK * c, BANK * (c + 1))

        def base(nb, c, z_bank):
            nc.tensor.matmul_mx(
                z_bank[:],
                lhsT=wb_codes[:, 2 * P * nb : 2 * P * (nb + 1)].bitcast(FP4X4),
                lhsT_scale=wb_sc[:, P * nb : P * (nb + 1)],
                rhs=xq_codes[:, 2 * BANK * c : 2 * BANK * (c + 1)].bitcast(FP4X4),
                rhs_scale=xq_sc[:, chunk(c)],
                start=True,
                stop=True,
            )

        def base_to_sbuf(nb, c):
            z_bank = rot.tile([P, BANK], F32, name="rot")
            base(nb, c, z_bank)
            nc.scalar.copy(z[nb][:, chunk(c)], z_bank[:])

        for c in range(CHUNKS):
            base_to_sbuf(0, c)

        part_a = held.tile([P, PACK, J], F32, name="part_a")
        part_b = held.tile([P, PACK, J], F32, name="part_b")

        def gather(part, plane, lst, share, j0, j1):
            nc.vector.tensor_tensor(
                part[:, plane, j0:j1],
                planes[plane][:].indirect(lst[:, j0 // PER_COLUMN : j1 // PER_COLUMN]),
                share[:, j0:j1],
                MULT,
            )

        merged = [held.tile([P, HALF, PACK], BF16, name=f"merged{h}", align_bytes=64) for h in range(2)]
        xm_codes = [held.tile([P, HALF], U32, name=f"xm_codes{h}", align_bytes=64) for h in range(2)]
        xm_sc = [held.tile([P, HALF], U8, name=f"xm_sc{h}", align_bytes=64) for h in range(2)]
        p_sb = [held.tile([P, J], F32, name=f"p_sb{nb}") for nb in range(ROW_BLOCKS)]

        def merge(h):
            cols = slice(HALF * h, HALF * (h + 1))
            nc.vector.tensor_tensor(
                merged[h][:].rearrange("p (c r) i -> p c i r", r=RUN),
                part_a[:, :, cols].rearrange("p i (c r) -> p c i r", r=RUN),
                part_b[:, :, cols].rearrange("p i (c r) -> p c i r", r=RUN),
                ADD,
            )

        def quantise(h):
            nc.vector.quantize_mx(
                xm_codes[h][:].bitcast(FP8X4), xm_sc[h][:], merged[h][:].rearrange("p j i -> p (j i)")
            )

        def product(h):
            for nb in range(ROW_BLOCKS):
                p_bank = rot.tile([P, HALF], F32, name="rot")
                nc.tensor.matmul_mx(
                    p_bank[:],
                    lhsT=wm_codes[:, P * nb : P * (nb + 1)].bitcast(FP8X4),
                    lhsT_scale=wm_sc[:, P * nb : P * (nb + 1)],
                    rhs=xm_codes[h][:].bitcast(FP8X4),
                    rhs_scale=xm_sc[h][:],
                    start=True,
                    stop=True,
                )
                nc.scalar.copy(p_sb[nb][:, HALF * h : HALF * (h + 1)], p_bank[:])

        last = PACK - 1
        for i in range(last):
            gather(part_a, i, list_a, share_a, 0, J)
            gather(part_b, i, list_b, share_b, 0, J)
        gather(part_a, last, list_a, share_a, 0, HALF)
        gather(part_b, last, list_b, share_b, 0, HALF)
        gather(part_a, last, list_a, share_a, HALF, J)
        merge(0)
        gather(part_b, last, list_b, share_b, HALF, J)
        quantise(0)
        product(0)
        merge(1)
        quantise(1)
        product(1)

        def scatter(nb, s, j0, j1):
            lst = (list_a, list_b)[s]
            nc.vector.tensor_copy(
                pages[nb][s][:].indirect(lst[:, j0 // PER_COLUMN : j1 // PER_COLUMN]), p_sb[nb][:, j0:j1]
            )

        for h in range(2):
            for s in range(2):
                scatter(0, s, HALF * h, HALF * (h + 1))
        for s in range(2):
            scatter(1, s, 0, J)

        for c in range(CHUNKS - 1):
            base_to_sbuf(1, c)
        z_last = keep.tile([P, BANK], F32, name="z_last")
        base(1, CHUNKS - 1, z_last)

        def add_turned(bank, src, c, first, final):
            for u in range(BLOCKS):
                col = BANK * c + P * u
                nc.tensor.matmul(
                    bank[:, u, :],
                    lhsT=src[:, col : col + P],
                    rhs=ident[:],
                    is_transpose=True,
                    start=(first and u == 0),
                    stop=(final and u == BLOCKS - 1),
                )

        def rows(nb, c):
            return out[P * nb : P * (nb + 1), chunk(c)]

        sums = [acc.tile([P, BLOCKS, P], F32, name="acc") for c in range(CHUNKS)]
        for c in range(CHUNKS):
            add_turned(sums[c], z[0], c, True, False)
        for c in range(CHUNKS):
            add_turned(sums[c], pages[0][0], c, False, False)
        for c in range(CHUNKS):
            add_turned(sums[c], pages[0][1], c, False, True)
        for c in range(CHUNKS):
            turned = stage.tile([P, BLOCKS, P], F32, name="turned")
            nc.scalar.copy(turned[:], sums[c][:])
            back = rot.tile([P, BLOCKS, P], F32, name="rot")
            for u in range(BLOCKS):
                nc.tensor.transpose(back[:, u, :], turned[:, u, :], ident[:])
            result = stage.tile([P, BANK], F32, name="result0")
            nc.scalar.copy(result[:], back[:].rearrange("p u q -> p (u q)"))
            nc.scalar.dma_start(out=rows(0, c), in_=result[:])

        partial = [stage.tile([P, BANK], F32, name="both") for c in range(CHUNKS)]
        for c in range(CHUNKS - 1):
            nc.gpsimd.tensor_tensor(partial[c][:], z[1][:, chunk(c)], pages[1][0][:, chunk(c)], ADD)
        nc.vector.tensor_tensor(partial[CHUNKS - 1][:], z_last[:], pages[1][0][:, chunk(CHUNKS - 1)], ADD)
        for c in range(CHUNKS):
            result = stage.tile([P, BANK], F32, name="result1")
            nc.vector.tensor_tensor(result[:], partial[c][:], pages[1][1][:, chunk(c)], ADD)
            nc.sync.dma_start(out=rows(1, c), in_=result[:])
